import numpy as np
import ml_dtypes


def mxq(x, axis, fmt="e4m3"):
    dtype, down = {"e4m3": (ml_dtypes.float8_e4m3fn, 7), "e5m2": (ml_dtypes.float8_e5m2, 14)}[fmt]
    v = np.moveaxis(np.asarray(x, np.float32).astype(ml_dtypes.bfloat16).astype(np.float64), axis, -1)
    blocks = v.reshape(v.shape[:-1] + (-1, 32))
    amax = np.abs(blocks).max(-1, keepdims=True)
    byte = np.maximum(np.where(amax > 0, np.frexp(amax)[1] - 1 + 127, 0) - down, 1)
    scale = np.exp2(byte - 127.0)
    codes = (blocks / scale).astype(np.float32).astype(dtype).astype(np.float64)
    return np.moveaxis((codes * scale).reshape(v.shape), -1, axis)


WIDE = False


def mx_kscale(k):
    if not WIDE:
        return np.ones(k)
    levels = np.array([10, -10, 5, -5, 0])
    if k % 512:
        return np.exp2(np.random.permutation(np.resize(levels, k // 32))).repeat(32)
    a = np.empty((k // 512, 16))
    for p in range(k // 512):
        a[p, :8] = np.random.permutation(np.resize(levels, 8))
        for g in range(8):
            far = levels[np.abs(levels - a[p, g]) >= 10]
            a[p, g + 8] = far[np.random.randint(len(far))]
    return np.exp2(a.ravel()).repeat(32)


def f64(x):
    return np.asarray(x).astype(np.float64)


def striped8(idx):
    return np.concatenate([x.reshape(-1, 16).T for x in idx]).astype(np.uint16)


def runs(offs, k):
    lists = np.stack([offs[16 * r : 16 * r + 16].T.reshape(-1) for r in range(8)]).astype(np.int64)
    return lists[np.arange(k) % 512 // 64]


def pack_weight(w):
    k, n = w.shape
    w = f64(np.asarray(w, np.float32).astype(ml_dtypes.bfloat16)).reshape(k // 32, 32, n)
    amax = np.abs(w).max(1)
    byte = np.clip(np.where(amax > 0, np.frexp(amax)[1] - 1 + 127 - 7, 1), 1, 254)
    scaled = (w * np.exp2(127.0 - byte)[:, None, :]).reshape(k, n).astype(np.float32)
    words = np.ascontiguousarray(scaled.reshape(k // 512, 128, 4, n).transpose(0, 1, 3, 2)).astype(ml_dtypes.float8_e4m3fn).view(np.uint8)
    return words, np.ascontiguousarray(byte.astype(np.uint8).reshape(k // 512, 16, n))


def unpack_weight(words, scales):
    g, p, n, _ = words.shape
    vals = np.ascontiguousarray(words).view(ml_dtypes.float8_e4m3fn).astype(np.float64) * np.repeat(np.exp2(scales.astype(np.float64) - 127.0), 8, axis=1)[..., None]
    return vals.transpose(0, 1, 3, 2).reshape(g * 512, n)


K, T, S, H = 512, 2048, 512, 512


def setup_inputs():
    n = np.random.standard_normal
    s = mx_kscale(K)[:, None]
    u = mx_kscale(H)
    packed_xT = pack_weight(n((K, T)) * s)
    return {
        "x_words": packed_xT[0],
        "x_scales": packed_xT[1],
        "w1": (n((K, H)) / np.sqrt(K) / s).astype(np.float32),
        "gn": (np.random.uniform(0.5, 1.5, (H, 1)) * u[:, None]).astype(np.float32),
        "dinv": np.random.uniform(0.3, 0.8, (H, S)).astype(np.float32),
        "w2": (n((H, H)) / np.sqrt(H) / u[:, None]).astype(np.float32),
        "offs": striped8(np.stack([np.random.permutation(T)[:S] for _ in range(8)])),
        "nb": striped8(np.stack([np.random.permutation(S) for _ in range(8)])),
    }


def reference(x_words, x_scales, w1, gn, dinv, w2, offs, nb):
    xq = unpack_weight(x_words, x_scales)[np.arange(K)[:, None], runs(offs, K)]
    y = mxq(f64(w1), 0, "e4m3").T @ xq
    z = f64(gn) * y
    w2q = mxq(f64(w2), 0, "e4m3")
    x1 = f64(dinv) * (y - (0.5 * ((w2q.T @ mxq(z, 0, "e4m3")))))
    z2 = f64(gn) * (x1[np.arange(H)[:, None], runs(nb, H)])
    return f64(dinv) * (y - (0.5 * ((w2q.T @ mxq(z2, 0, "e4m3")))))

@@ -1,0 +1,217 @@
+from contextlib import ExitStack
+
+import concourse.mybir as mybir
+
+K, T, S, H = 512, 2048, 512, 512
+FLOPS = 3 * 2 * 512 * 512 * 512
+
+F32 = mybir.dt.float32
+BF16 = mybir.dt.bfloat16
+I32 = mybir.dt.int32
+U32 = mybir.dt.uint32
+U16 = mybir.dt.uint16
+U8 = mybir.dt.uint8
+FP8X4 = mybir.dt.float8_e4m3fn_x4
+MULT = mybir.AluOpType.mult
+ADD = mybir.AluOpType.add
+
+P = 128
+PACK = 4
+HALF = S // 2
+QUARTER = S // 4
+PER_COL = 16
+
+
+def tile_picked_jacobi2_none_p_kernel(
+    tc, x_words, x_scales, w1, gn, dinv, w2, offs, nb, out
+):
+    nc = tc.nc
+    with ExitStack() as ctx:
+        keep = ctx.enter_context(tc.tile_pool(name="keep", bufs=1))
+        psum = ctx.enter_context(tc.psum_pool(name="psum", bufs=1))
+
+        def sb(name, shape, dtype):
+            return keep.tile(shape, dtype, name=name, align_bytes=64)
+
+        def bank(index, shape):
+            return psum.tile(shape, F32, name="bank%d" % index)
+
+        def mx(acc, w_codes, w_scales, t, codes, scales, cols, start, stop):
+            rows = slice(t * P, (t + 1) * P)
+            nc.tensor.matmul_mx(
+                out=acc,
+                lhsT=w_codes[:, rows].bitcast(FP8X4),
+                lhsT_scale=w_scales[:, rows],
+                rhs=codes[:, cols].bitcast(FP8X4),
+                rhs_scale=scales[:, cols],
+                start=start,
+                stop=stop,
+            )
+
+        offs_t = keep.tile([P, S // PER_COL], U16, name="offs_t")
+        nb_t = keep.tile([P, S // PER_COL], U16, name="nb_t")
+        nc.sync.dma_start(offs_t[:], offs)
+        nc.sync.dma_start(nb_t[:], nb)
+
+        scale_win = sb("scale_win", [P, T], U8)
+        nc.vector.memset(scale_win[:].bitcast(I32), 0)
+        nc.scalar.dma_start(scale_win[0:P:8, :].bitcast(I32), x_scales[0].bitcast(I32))
+
+        w1_raw = sb("w1_raw", [P, PACK, H], F32)
+        nc.sync.dma_start(w1_raw[:], w1.rearrange("(p j) c -> p j c", j=PACK))
+        word_win = sb("word_win", [P, T], I32)
+        nc.sync.dma_start(word_win[:], x_words[0].rearrange("p n r -> p (n r)").bitcast(I32))
+        w2_rows = w2.rearrange("(p j) c -> p j c", j=PACK)
+        w2_raw = [sb("w2_raw%d" % h, [P, PACK, H // 2], F32) for h in range(2)]
+        for h in range(2):
+            nc.sync.dma_start(w2_raw[h][:], w2_rows[:, :, h * (H // 2) : (h + 1) * (H // 2)])
+        dinv_t = sb("dinv_t", [P, PACK, S], F32)
+        nc.sync.dma_start(dinv_t[:], dinv.rearrange("(p t) n -> p t n", t=PACK))
+
+        gn_t = sb("gn_t", [P, PACK], F32)
+        nc.gpsimd.dma_start(gn_t[:], gn.rearrange("(p t) o -> p (t o)", t=PACK))
+        gain = sb("gain", [P, PACK], F32)
+        nc.gpsimd.tensor_scalar(gain[:], gn_t[:], -0.5, 0.0, MULT, ADD)
+
+        scale_got = sb("scale_got", [P, S], U8)
+        nc.vector.tensor_copy(scale_got[:], scale_win[:].indirect(offs_t[:]))
+        x_sc = sb("x_sc", [P, S], U8)
+        nc.vector.tensor_copy(x_sc[:].bitcast(I32), scale_got[:].bitcast(I32))
+        for c in range(1, 4):
+            nc.scalar.dma_start(x_sc[c:P:32, :].bitcast(I32), scale_got[8 * c : P : 32, :].bitcast(I32))
+
+        w1_bf = sb("w1_bf", [P, H * PACK], BF16)
+        nc.vector.tensor_copy(
+            w1_bf[:].rearrange("p (t m j) -> p m t j", t=PACK, j=PACK),
+            w1_raw[:].rearrange("p j (m t) -> p m t j", t=PACK),
+        )
+        w1_q = sb("w1_q", [P, H], U32)
+        w1_s = sb("w1_s", [P, H], U8)
+        nc.vector.quantize_mx(out=w1_q[:].bitcast(FP8X4), scales=w1_s[:], in_=w1_bf[:])
+
+        x_q = sb("x_q", [P, S], U32)
+        for h in range(2):
+            lists = offs_t[:, h * HALF // PER_COL : (h + 1) * HALF // PER_COL]
+            nc.vector.tensor_copy(x_q[:, h * HALF : (h + 1) * HALF], word_win[:].bitcast(U32).indirect(lists))
+
+        w2_bf = sb("w2_bf", [P, H * PACK], BF16)
+        w2_dst = w2_bf[:].rearrange("p (t m j) -> p m t j", t=PACK, j=PACK)
+        for h in range(2):
+            nc.scalar.copy(
+                w2_dst[:, h * (P // 2) : (h + 1) * (P // 2)],
+                w2_raw[h][:].rearrange("p j (m t) -> p m t j", t=PACK),
+            )
+        w2_s = sb("w2_s", [P, H], U8)
+
+        y_ps = [bank(c, [P, PACK, QUARTER]) for c in range(4)]
+        for c in range(4):
+            for t in range(PACK):
+                mx(y_ps[c][:, t, :], w1_q, w1_s, t, x_q, x_sc, slice(c * QUARTER, (c + 1) * QUARTER), True, True)
+
+        z_bf = [
+            keep.tile([P, HALF * PACK], BF16, name="z_bf0", tag="z0_then_w2", align_bytes=64),
+            sb("z_bf1", [P, HALF * PACK], BF16),
+        ]
+        z_q = sb("z_q", [P, S], U32)
+        z_s = sb("z_s", [P, S], U8)
+        y_sb = sb("y_sb", [P, PACK, S], F32)
+        gain_b = gain[:].unsqueeze(1).to_broadcast([P, QUARTER, PACK])
+
+        def make_z(c):
+            dst = z_bf[c // 2][:, c % 2 * QUARTER * PACK : (c % 2 + 1) * QUARTER * PACK].rearrange("p (n t) -> p n t", t=PACK)
+            nc.vector.tensor_tensor(dst, y_ps[c][:].rearrange("p t n -> p n t"), gain_b, MULT)
+            nc.scalar.copy(y_sb[:, :, c * QUARTER : (c + 1) * QUARTER], y_ps[c][:])
+
+        def quantize_half(codes, scales, values, h):
+            cols = slice(h * HALF, (h + 1) * HALF)
+            nc.vector.quantize_mx(out=codes[:, cols].bitcast(FP8X4), scales=scales[:, cols], in_=values)
+
+        make_z(0)
+        make_z(1)
+        make_z(2)
+        quantize_half(z_q, z_s, z_bf[0][:], 0)
+        w2_q = keep.tile([P, H], U32, name="w2_q", tag="z0_then_w2", align_bytes=64)
+        nc.vector.quantize_mx(out=w2_q[:].bitcast(FP8X4), scales=w2_s[:], in_=w2_bf[:])
+        make_z(3)
+        quantize_half(z_q, z_s, z_bf[1][:], 1)
+
+        r1 = [bank(4 + t, [P, S]) for t in range(PACK)]
+        win = [sb("win%d" % t, [P, S], F32) for t in range(PACK)]
+        last = sb("last", [P, S], F32)
+
+        def first_product(t, h):
+            cols = slice(h * HALF, (h + 1) * HALF)
+            if t < PACK - 1:
+                mx(r1[t][:, cols], w1_q, w1_s, t, x_q, x_sc, cols, True, False)
+            mx(r1[t][:, cols], w2_q, w2_s, t, z_q, z_s, cols, t == PACK - 1, True)
+
+        def first_sum(h):
+            cols = slice(h * HALF, (h + 1) * HALF)
+            nc.vector.tensor_tensor(last[:, cols], r1[PACK - 1][:, cols], y_sb[:, PACK - 1, cols], ADD)
+
+        def first_values(t, h):
+            cols = slice(h * HALF, (h + 1) * HALF)
+            rest = r1[t][:, cols] if t < PACK - 1 else last[:, cols]
+            nc.vector.scalar_tensor_tensor(win[t][:, cols], rest, gain[:, t : t + 1], dinv_t[:, t, cols], MULT, MULT)
+
+        for t in range(PACK):
+            first_product(t, 0)
+        for h in range(2):
+            for t in range(PACK):
+                if t == 1:
+                    first_sum(h)
+                first_values(t, h)
+                if h == 0:
+                    first_product(t, 1)
+
+        got0 = sb("got0", [P, PACK, HALF], BF16)
+        shared = sb("shared", [P, (2 * PACK - 1) * HALF], BF16)
+        woven0 = shared[:, (PACK - 1) * HALF :]
+        got1 = shared[:, : PACK * HALF].rearrange("p (t n) -> p t n", t=PACK)
+        woven1 = sb("woven1", [P, PACK * HALF], BF16)
+        z2_q = sb("z2_q", [P, S], U32)
+        z2_s = sb("z2_s", [P, S], U8)
+
+        def fetch(dst, t, h):
+            lists = nb_t[:, h * HALF // PER_COL : (h + 1) * HALF // PER_COL]
+            nc.vector.tensor_copy(dst, win[t][:].indirect(lists))
+
+        for t in range(PACK):
+            fetch(got0[:, t, :], t, 0)
+        nc.scalar.copy(woven0.rearrange("p (n t) -> p n t", t=PACK), got0[:].rearrange("p t n -> p n t"))
+        for t in range(PACK - 1):
+            fetch(got1[:, t, :], t, 1)
+        quantize_half(z2_q, z2_s, woven0, 0)
+        fetch(got1[:, PACK - 1, :], PACK - 1, 1)
+        nc.scalar.copy(woven1[:].rearrange("p (n t) -> p n t", t=PACK), got1.rearrange("p t n -> p n t"))
+
+        out_rows = out.rearrange("(p t) n -> p t n", t=PACK)
+        r2 = [[bank(2 * h + u, [P, 2, HALF]) for u in range(2)] for h in range(2)]
+        rest2 = [[sb("rest%d%d" % (h, u), [P, 2, HALF], F32) for u in range(2)] for h in range(2)]
+        res = [[sb("res%d%d" % (h, u), [P, 2, HALF], F32) for u in range(2)] for h in range(2)]
+
+        def product(h):
+            cols = slice(h * HALF, (h + 1) * HALF)
+            for t in range(PACK):
+                mx(r2[h][t // 2][:, t % 2, :], w2_q, w2_s, t, z2_q, z2_s, cols, True, True)
+
+        def subtract(h, u):
+            cols = slice(h * HALF, (h + 1) * HALF)
+            nc.vector.tensor_tensor(rest2[h][u][:], r2[h][u][:], y_sb[:, 2 * u : 2 * u + 2, cols], ADD)
+
+        def finish(h, u):
+            cols = slice(h * HALF, (h + 1) * HALF)
+            nc.vector.tensor_tensor(res[h][u][:], rest2[h][u][:], dinv_t[:, 2 * u : 2 * u + 2, cols], MULT)
+            nc.sync.dma_start(out_rows[:, 2 * u : 2 * u + 2, cols], res[h][u][:])
+
+        product(0)
+        subtract(0, 0)
+        subtract(0, 1)
+        quantize_half(z2_q, z2_s, woven1[:], 1)
+        product(1)
+        finish(0, 0)
+        finish(0, 1)
+        subtract(1, 0)
+        subtract(1, 1)
+        finish(1, 0)
+        finish(1, 1)

@@ -50,40 +50,44 @@ def tile_picked_jacobi2_none_p_kernel(
 
         offs_t = keep.tile([P, S // PER_COL], U16, name="offs_t")
         nb_t = keep.tile([P, S // PER_COL], U16, name="nb_t")
+        scale_win = keep.tile([P, T], U8, name="scale_win", tag="scales_then_late", align_bytes=64)
+        nc.vector.memset(scale_win[:, : T // 2].bitcast(I32), 0)
+        nc.gpsimd.memset(scale_win[:, T // 2 :].bitcast(I32), 0)
+        x_sc = sb("x_sc", [P, S], U8)
+
         nc.sync.dma_start(offs_t[:], offs)
-        nc.sync.dma_start(nb_t[:], nb)
-
-        scale_win = sb("scale_win", [P, T], U8)
-        nc.vector.memset(scale_win[:].bitcast(I32), 0)
-        nc.scalar.dma_start(scale_win[0:P:8, :].bitcast(I32), x_scales[0].bitcast(I32))
-
-        w1_raw = sb("w1_raw", [P, PACK, H], F32)
-        nc.sync.dma_start(w1_raw[:], w1.rearrange("(p j) c -> p j c", j=PACK))
+        w1_raw = sb("w1_raw", [P, PACK * H], F32)
+        w1_rows = w1.rearrange("(p j) c -> p (j c)", j=PACK)
+        nc.sync.dma_start(w1_raw[:, : 2 * H], w1_rows[:, : 2 * H])
+        nc.sync.dma_start(scale_win[0:P:8, :].bitcast(I32), x_scales[0].bitcast(I32))
+        nc.sync.dma_start(w1_raw[:, 2 * H :], w1_rows[:, 2 * H :])
         word_win = sb("word_win", [P, T], I32)
         nc.sync.dma_start(word_win[:], x_words[0].rearrange("p n r -> p (n r)").bitcast(I32))
         w2_rows = w2.rearrange("(p j) c -> p j c", j=PACK)
-        w2_raw = [sb("w2_raw%d" % h, [P, PACK, H // 2], F32) for h in range(2)]
-        for h in range(2):
-            nc.sync.dma_start(w2_raw[h][:], w2_rows[:, :, h * (H // 2) : (h + 1) * (H // 2)])
-        dinv_t = sb("dinv_t", [P, PACK, S], F32)
-        nc.sync.dma_start(dinv_t[:], dinv.rearrange("(p t) n -> p t n", t=PACK))
-
+        w2_first = sb("w2_first", [P, PACK, H // 2], F32)
+        nc.sync.dma_start(w2_first[:], w2_rows[:, :, : H // 2])
+        nc.sync.dma_start(nb_t[:], nb)
         gn_t = sb("gn_t", [P, PACK], F32)
         nc.gpsimd.dma_start(gn_t[:], gn.rearrange("(p t) o -> p (t o)", t=PACK))
+
         gain = sb("gain", [P, PACK], F32)
         nc.gpsimd.tensor_scalar(gain[:], gn_t[:], -0.5, 0.0, MULT, ADD)
 
         scale_got = sb("scale_got", [P, S], U8)
         nc.vector.tensor_copy(scale_got[:], scale_win[:].indirect(offs_t[:]))
-        x_sc = sb("x_sc", [P, S], U8)
-        nc.vector.tensor_copy(x_sc[:].bitcast(I32), scale_got[:].bitcast(I32))
-        for c in range(1, 4):
+        for c in range(4):
             nc.scalar.dma_start(x_sc[c:P:32, :].bitcast(I32), scale_got[8 * c : P : 32, :].bitcast(I32))
+
+        late = keep.tile([P, 6 * H], F32, name="late", tag="scales_then_late", align_bytes=64)
+        w2_raw = [w2_first[:], late[:, : 2 * H].rearrange("p (j c) -> p j c", j=PACK)]
+        nc.sync.dma_start(w2_raw[1], w2_rows[:, :, H // 2 :])
+        dinv_t = late[:, 2 * H :].rearrange("p (t n) -> p t n", t=PACK)
+        nc.sync.dma_start(dinv_t, dinv.rearrange("(p t) n -> p t n", t=PACK))
 
         w1_bf = sb("w1_bf", [P, H * PACK], BF16)
         nc.vector.tensor_copy(
             w1_bf[:].rearrange("p (t m j) -> p m t j", t=PACK, j=PACK),
-            w1_raw[:].rearrange("p j (m t) -> p m t j", t=PACK),
+            w1_raw[:].rearrange("p (j m t) -> p m t j", j=PACK, t=PACK),
         )
         w1_q = sb("w1_q", [P, H], U32)
         w1_s = sb("w1_s", [P, H], U8)
@@ -99,7 +103,7 @@ def tile_picked_jacobi2_none_p_kernel(
         for h in range(2):
             nc.scalar.copy(
                 w2_dst[:, h * (P // 2) : (h + 1) * (P // 2)],
-                w2_raw[h][:].rearrange("p j (m t) -> p m t j", t=PACK),
+                w2_raw[h].rearrange("p j (m t) -> p m t j", t=PACK),
             )
         w2_s = sb("w2_s", [P, H], U8)
 
@@ -107,6 +111,10 @@ def tile_picked_jacobi2_none_p_kernel(
         for c in range(4):
             for t in range(PACK):
                 mx(y_ps[c][:, t, :], w1_q, w1_s, t, x_q, x_sc, slice(c * QUARTER, (c + 1) * QUARTER), True, True)
+
+        r1 = [bank(4 + t, [P, S]) for t in range(PACK)]
+        for t in range(PACK - 1):
+            mx(r1[t][:], w1_q, w1_s, t, x_q, x_sc, slice(0, S), True, False)
 
         z_bf = [
             keep.tile([P, HALF * PACK], BF16, name="z_bf0", tag="z0_then_w2", align_bytes=64),
@@ -135,34 +143,33 @@ def tile_picked_jacobi2_none_p_kernel(
         make_z(3)
         quantize_half(z_q, z_s, z_bf[1][:], 1)
 
-        r1 = [bank(4 + t, [P, S]) for t in range(PACK)]
+        LAST = PACK - 1
         win = [sb("win%d" % t, [P, S], F32) for t in range(PACK)]
         last = sb("last", [P, S], F32)
 
         def first_product(t, h):
             cols = slice(h * HALF, (h + 1) * HALF)
-            if t < PACK - 1:
-                mx(r1[t][:, cols], w1_q, w1_s, t, x_q, x_sc, cols, True, False)
-            mx(r1[t][:, cols], w2_q, w2_s, t, z_q, z_s, cols, t == PACK - 1, True)
+            mx(r1[t][:, cols], w2_q, w2_s, t, z_q, z_s, cols, t == LAST, t == LAST or h == 1)
 
-        def first_sum(h):
-            cols = slice(h * HALF, (h + 1) * HALF)
-            nc.vector.tensor_tensor(last[:, cols], r1[PACK - 1][:, cols], y_sb[:, PACK - 1, cols], ADD)
+        def first_sum(cols):
+            nc.vector.tensor_tensor(last[:, cols], r1[LAST][:, cols], y_sb[:, LAST, cols], ADD)
 
-        def first_values(t, h):
-            cols = slice(h * HALF, (h + 1) * HALF)
-            rest = r1[t][:, cols] if t < PACK - 1 else last[:, cols]
+        def first_values(t, cols):
+            rest = r1[t][:, cols] if t < LAST else last[:, cols]
             nc.vector.scalar_tensor_tensor(win[t][:, cols], rest, gain[:, t : t + 1], dinv_t[:, t, cols], MULT, MULT)
 
-        for t in range(PACK):
-            first_product(t, 0)
+        first_product(LAST, 0)
         for h in range(2):
-            for t in range(PACK):
-                if t == 1:
-                    first_sum(h)
-                first_values(t, h)
-                if h == 0:
-                    first_product(t, 1)
+            for t in range(LAST):
+                first_product(t, h)
+        first_sum(slice(0, HALF))
+        first_values(LAST, slice(0, HALF))
+        first_product(LAST, 1)
+        first_values(0, slice(0, S))
+        first_values(1, slice(0, S))
+        first_sum(slice(HALF, S))
+        first_values(2, slice(0, S))
+        first_values(LAST, slice(HALF, S))
 
         got0 = sb("got0", [P, PACK, HALF], BF16)
         shared = sb("shared", [P, (2 * PACK - 1) * HALF], BF16)
@@ -199,10 +206,11 @@ def tile_picked_jacobi2_none_p_kernel(
             cols = slice(h * HALF, (h + 1) * HALF)
             nc.vector.tensor_tensor(rest2[h][u][:], r2[h][u][:], y_sb[:, 2 * u : 2 * u + 2, cols], ADD)
 
-        def finish(h, u):
+        def finish(h, u, lo=0, hi=2):
             cols = slice(h * HALF, (h + 1) * HALF)
-            nc.vector.tensor_tensor(res[h][u][:], rest2[h][u][:], dinv_t[:, 2 * u : 2 * u + 2, cols], MULT)
-            nc.sync.dma_start(out_rows[:, 2 * u : 2 * u + 2, cols], res[h][u][:])
+            planes = slice(2 * u + lo, 2 * u + hi)
+            nc.vector.tensor_tensor(res[h][u][:, lo:hi], rest2[h][u][:, lo:hi], dinv_t[:, planes, cols], MULT)
+            nc.sync.dma_start(out_rows[:, planes, cols], res[h][u][:, lo:hi])
 
         product(0)
         subtract(0, 0)
@@ -214,4 +222,5 @@ def tile_picked_jacobi2_none_p_kernel(
         subtract(1, 0)
         subtract(1, 1)
         finish(1, 0)
-        finish(1, 1)
+        finish(1, 1, 0, 1)
+        finish(1, 1, 1, 2)

@@ -14,6 +14,7 @@ U8 = mybir.dt.uint8
 FP8X4 = mybir.dt.float8_e4m3fn_x4
 MULT = mybir.AluOpType.mult
 ADD = mybir.AluOpType.add
+COPY = mybir.ActivationFunctionType.Copy
 
 P = 128
 PACK = 4
@@ -28,6 +29,7 @@ def tile_picked_jacobi2_none_p_kernel(
     nc = tc.nc
     with ExitStack() as ctx:
         keep = ctx.enter_context(tc.tile_pool(name="keep", bufs=1))
+        reuse = ctx.enter_context(tc.tile_pool(name="reuse", bufs=1))
         psum = ctx.enter_context(tc.psum_pool(name="psum", bufs=1))
 
         def sb(name, shape, dtype):
@@ -50,25 +52,22 @@ def tile_picked_jacobi2_none_p_kernel(
 
         offs_t = keep.tile([P, S // PER_COL], U16, name="offs_t")
         nb_t = keep.tile([P, S // PER_COL], U16, name="nb_t")
-        scale_win = keep.tile([P, T], U8, name="scale_win", tag="scales_then_late", align_bytes=64)
+        scale_win = reuse.tile([P, T], U8, name="scale_win", offset=3072)
         nc.vector.memset(scale_win[:, : T // 2].bitcast(I32), 0)
         nc.gpsimd.memset(scale_win[:, T // 2 :].bitcast(I32), 0)
         x_sc = sb("x_sc", [P, S], U8)
 
         nc.sync.dma_start(offs_t[:], offs)
-        w1_raw = sb("w1_raw", [P, PACK * H], F32)
+        w1_raw = reuse.tile([P, PACK * H], F32, name="w1_raw", offset=8192)
         w1_rows = w1.rearrange("(p j) c -> p (j c)", j=PACK)
-        nc.sync.dma_start(w1_raw[:, : 2 * H], w1_rows[:, : 2 * H])
+        nc.sync.dma_start(w1_raw[:, :H], w1_rows[:, :H])
+        gn_t = sb("gn_t", [P, PACK], F32)
+        nc.sync.dma_start(gn_t[:], gn.rearrange("(p t) o -> p (t o)", t=PACK))
+        nc.sync.dma_start(nb_t[:], nb)
         nc.sync.dma_start(scale_win[0:P:8, :].bitcast(I32), x_scales[0].bitcast(I32))
-        nc.sync.dma_start(w1_raw[:, 2 * H :], w1_rows[:, 2 * H :])
+        nc.sync.dma_start(w1_raw[:, H:], w1_rows[:, H:])
         word_win = sb("word_win", [P, T], I32)
         nc.sync.dma_start(word_win[:], x_words[0].rearrange("p n r -> p (n r)").bitcast(I32))
-        w2_rows = w2.rearrange("(p j) c -> p j c", j=PACK)
-        w2_first = sb("w2_first", [P, PACK, H // 2], F32)
-        nc.sync.dma_start(w2_first[:], w2_rows[:, :, : H // 2])
-        nc.sync.dma_start(nb_t[:], nb)
-        gn_t = sb("gn_t", [P, PACK], F32)
-        nc.gpsimd.dma_start(gn_t[:], gn.rearrange("(p t) o -> p (t o)", t=PACK))
 
         gain = sb("gain", [P, PACK], F32)
         nc.gpsimd.tensor_scalar(gain[:], gn_t[:], -0.5, 0.0, MULT, ADD)
@@ -76,19 +75,21 @@ def tile_picked_jacobi2_none_p_kernel(
         scale_got = sb("scale_got", [P, S], U8)
         nc.vector.tensor_copy(scale_got[:], scale_win[:].indirect(offs_t[:]))
         for c in range(4):
-            nc.scalar.dma_start(x_sc[c:P:32, :].bitcast(I32), scale_got[8 * c : P : 32, :].bitcast(I32))
+            queue = nc.sync if c % 2 else nc.scalar
+            queue.dma_start(x_sc[c:P:32, :].bitcast(I32), scale_got[8 * c : P : 32, :].bitcast(I32))
 
-        late = keep.tile([P, 6 * H], F32, name="late", tag="scales_then_late", align_bytes=64)
-        w2_raw = [w2_first[:], late[:, : 2 * H].rearrange("p (j c) -> p j c", j=PACK)]
-        nc.sync.dma_start(w2_raw[1], w2_rows[:, :, H // 2 :])
-        dinv_t = late[:, 2 * H :].rearrange("p (t n) -> p t n", t=PACK)
-        nc.sync.dma_start(dinv_t, dinv.rearrange("(p t) n -> p t n", t=PACK))
+        w2_rows = w2.rearrange("(p j) c -> p j c", j=PACK)
+        w2_raw = [reuse.tile([P, PACK, H // 2], F32, name="w2_raw%d" % h, offset=4096 * h) for h in range(2)]
+        for h in range(2):
+            nc.sync.dma_start(w2_raw[h][:], w2_rows[:, :, h * (H // 2) : (h + 1) * (H // 2)])
 
         w1_bf = sb("w1_bf", [P, H * PACK], BF16)
         nc.vector.tensor_copy(
             w1_bf[:].rearrange("p (t m j) -> p m t j", t=PACK, j=PACK),
             w1_raw[:].rearrange("p (j m t) -> p m t j", j=PACK, t=PACK),
         )
+        dinv_t = reuse.tile([P, PACK, S], F32, name="dinv_t", offset=8192)
+        nc.sync.dma_start(dinv_t[:], dinv.rearrange("(p t) n -> p t n", t=PACK))
         w1_q = sb("w1_q", [P, H], U32)
         w1_s = sb("w1_s", [P, H], U8)
         nc.vector.quantize_mx(out=w1_q[:].bitcast(FP8X4), scales=w1_s[:], in_=w1_bf[:])
@@ -98,12 +99,13 @@ def tile_picked_jacobi2_none_p_kernel(
             lists = offs_t[:, h * HALF // PER_COL : (h + 1) * HALF // PER_COL]
             nc.vector.tensor_copy(x_q[:, h * HALF : (h + 1) * HALF], word_win[:].bitcast(U32).indirect(lists))
 
-        w2_bf = sb("w2_bf", [P, H * PACK], BF16)
-        w2_dst = w2_bf[:].rearrange("p (t m j) -> p m t j", t=PACK, j=PACK)
+        stage = sb("stage", [P, (QUARTER + H) * PACK], BF16)
+        w2_bf = stage[:, QUARTER * PACK :]
+        w2_dst = w2_bf.rearrange("p (t m j) -> p m t j", t=PACK, j=PACK)
         for h in range(2):
             nc.scalar.copy(
                 w2_dst[:, h * (P // 2) : (h + 1) * (P // 2)],
-                w2_raw[h].rearrange("p j (m t) -> p m t j", t=PACK),
+                w2_raw[h][:].rearrange("p j (m t) -> p m t j", t=PACK),
             )
         w2_s = sb("w2_s", [P, H], U8)
 
@@ -117,12 +119,12 @@ def tile_picked_jacobi2_none_p_kernel(
             mx(r1[t][:], w1_q, w1_s, t, x_q, x_sc, slice(0, S), True, False)
 
         z_bf = [
-            keep.tile([P, HALF * PACK], BF16, name="z_bf0", tag="z0_then_w2", align_bytes=64),
-            sb("z_bf1", [P, HALF * PACK], BF16),
+            keep.tile([P, HALF * PACK], BF16, name="z_bf0", tag="z0_then_w2", align_bytes=64)[:],
+            stage[:, : HALF * PACK],
         ]
         z_q = sb("z_q", [P, S], U32)
         z_s = sb("z_s", [P, S], U8)
-        y_sb = sb("y_sb", [P, PACK, S], F32)
+        y_sb = reuse.tile([P, PACK, S], F32, name="y_sb", offset=0)
         gain_b = gain[:].unsqueeze(1).to_broadcast([P, QUARTER, PACK])
 
         def make_z(c):
@@ -137,11 +139,11 @@ def tile_picked_jacobi2_none_p_kernel(
         make_z(0)
         make_z(1)
         make_z(2)
-        quantize_half(z_q, z_s, z_bf[0][:], 0)
+        quantize_half(z_q, z_s, z_bf[0], 0)
         w2_q = keep.tile([P, H], U32, name="w2_q", tag="z0_then_w2", align_bytes=64)
-        nc.vector.quantize_mx(out=w2_q[:].bitcast(FP8X4), scales=w2_s[:], in_=w2_bf[:])
+        nc.vector.quantize_mx(out=w2_q[:].bitcast(FP8X4), scales=w2_s[:], in_=w2_bf)
         make_z(3)
-        quantize_half(z_q, z_s, z_bf[1][:], 1)
+        quantize_half(z_q, z_s, z_bf[1], 1)
 
         LAST = PACK - 1
         win = [sb("win%d" % t, [P, S], F32) for t in range(PACK)]
@@ -158,21 +160,27 @@ def tile_picked_jacobi2_none_p_kernel(
             rest = r1[t][:, cols] if t < LAST else last[:, cols]
             nc.vector.scalar_tensor_tensor(win[t][:, cols], rest, gain[:, t : t + 1], dinv_t[:, t, cols], MULT, MULT)
 
-        first_product(LAST, 0)
-        for h in range(2):
-            for t in range(LAST):
-                first_product(t, h)
+        shared = sb("shared", [P, (2 * PACK - 1) * HALF], BF16)
+        scaled = [sb("scaled", [P, S], F32)[:], shared[:, HALF : HALF + 2 * S].bitcast(F32)]
+
+        def first_values_aside(t):
+            nc.scalar.activation(scaled[t - 1], r1[t][:], COPY, scale=gain[:, t : t + 1])
+            nc.gpsimd.tensor_tensor(win[t][:], scaled[t - 1], dinv_t[:, t, :], MULT)
+
+        for t in (LAST, 1, 0, 2):
+            first_product(t, 0)
+        for t in (1, 0, 2):
+            first_product(t, 1)
         first_sum(slice(0, HALF))
         first_values(LAST, slice(0, HALF))
         first_product(LAST, 1)
+        first_values_aside(1)
+        first_values_aside(2)
         first_values(0, slice(0, S))
-        first_values(1, slice(0, S))
         first_sum(slice(HALF, S))
-        first_values(2, slice(0, S))
         first_values(LAST, slice(HALF, S))
 
         got0 = sb("got0", [P, PACK, HALF], BF16)
-        shared = sb("shared", [P, (2 * PACK - 1) * HALF], BF16)
         woven0 = shared[:, (PACK - 1) * HALF :]
         got1 = shared[:, : PACK * HALF].rearrange("p (t n) -> p t n", t=PACK)
         woven1 = sb("woven1", [P, PACK * HALF], BF16)
@@ -183,7 +191,7 @@ def tile_picked_jacobi2_none_p_kernel(
             lists = nb_t[:, h * HALF // PER_COL : (h + 1) * HALF // PER_COL]
             nc.vector.tensor_copy(dst, win[t][:].indirect(lists))
 
-        for t in range(PACK):
+        for t in (0, 3, 1, 2):
             fetch(got0[:, t, :], t, 0)
         nc.scalar.copy(woven0.rearrange("p (n t) -> p n t", t=PACK), got0[:].rearrange("p t n -> p n t"))
         for t in range(PACK - 1):
@@ -195,7 +203,6 @@ def tile_picked_jacobi2_none_p_kernel(
         out_rows = out.rearrange("(p t) n -> p t n", t=PACK)
         r2 = [[bank(2 * h + u, [P, 2, HALF]) for u in range(2)] for h in range(2)]
         rest2 = [[sb("rest%d%d" % (h, u), [P, 2, HALF], F32) for u in range(2)] for h in range(2)]
-        res = [[sb("res%d%d" % (h, u), [P, 2, HALF], F32) for u in range(2)] for h in range(2)]
 
         def product(h):
             cols = slice(h * HALF, (h + 1) * HALF)
@@ -206,21 +213,22 @@ def tile_picked_jacobi2_none_p_kernel(
             cols = slice(h * HALF, (h + 1) * HALF)
             nc.vector.tensor_tensor(rest2[h][u][:], r2[h][u][:], y_sb[:, 2 * u : 2 * u + 2, cols], ADD)
 
-        def finish(h, u, lo=0, hi=2):
+        def finish(engine, res, h, u, lo=0, hi=2):
             cols = slice(h * HALF, (h + 1) * HALF)
             planes = slice(2 * u + lo, 2 * u + hi)
-            nc.vector.tensor_tensor(res[h][u][:, lo:hi], rest2[h][u][:, lo:hi], dinv_t[:, planes, cols], MULT)
-            nc.sync.dma_start(out_rows[:, planes, cols], res[h][u][:, lo:hi])
+            engine.tensor_tensor(res[:, lo:hi], rest2[h][u][:, lo:hi], dinv_t[:, planes, cols], MULT)
+            nc.sync.dma_start(out_rows[:, planes, cols], res[:, lo:hi])
 
         product(0)
         subtract(0, 0)
         subtract(0, 1)
         quantize_half(z2_q, z2_s, woven1[:], 1)
         product(1)
-        finish(0, 0)
-        finish(0, 1)
+        finish(nc.vector, sb("woven1", [P, 2, HALF], F32), 0, 0)
+        finish(nc.gpsimd, sb("rest00", [P, 2, HALF], F32), 0, 1)
         subtract(1, 0)
         subtract(1, 1)
-        finish(1, 0)
-        finish(1, 1, 0, 1)
-        finish(1, 1, 1, 2)
+        finish(nc.vector, sb("res10", [P, 2, HALF], F32), 1, 0)
+        res11 = sb("res11", [P, 2, HALF], F32)
+        finish(nc.vector, res11, 1, 1, 0, 1)
+        finish(nc.vector, res11, 1, 1, 1, 2)

@@ -21,6 +21,7 @@ PACK = 4
 HALF = S // 2
 QUARTER = S // 4
 PER_COL = 16
+W1_SPLIT = 80
 
 
 def tile_picked_jacobi2_none_p_kernel(
@@ -38,14 +39,14 @@ def tile_picked_jacobi2_none_p_kernel(
         def bank(index, shape):
             return psum.tile(shape, F32, name="bank%d" % index)
 
-        def mx(acc, w_codes, w_scales, t, codes, scales, cols, start, stop):
+        def mx(acc, w_codes, w_scales, t, codes, scales, start, stop):
             rows = slice(t * P, (t + 1) * P)
             nc.tensor.matmul_mx(
                 out=acc,
                 lhsT=w_codes[:, rows].bitcast(FP8X4),
                 lhsT_scale=w_scales[:, rows],
-                rhs=codes[:, cols].bitcast(FP8X4),
-                rhs_scale=scales[:, cols],
+                rhs=codes.bitcast(FP8X4),
+                rhs_scale=scales,
                 start=start,
                 stop=stop,
             )
@@ -70,7 +71,7 @@ def tile_picked_jacobi2_none_p_kernel(
         nc.sync.dma_start(word_win[:], x_words[0].rearrange("p n r -> p (n r)").bitcast(I32))
 
         gain = sb("gain", [P, PACK], F32)
-        nc.gpsimd.tensor_scalar(gain[:], gn_t[:], -0.5, 0.0, MULT, ADD)
+        nc.scalar.activation(gain[:], gn_t[:], COPY, scale=-0.5)
 
         scale_got = sb("scale_got", [P, S], U8)
         nc.vector.tensor_copy(scale_got[:], scale_win[:].indirect(offs_t[:]))
@@ -84,10 +85,10 @@ def tile_picked_jacobi2_none_p_kernel(
             nc.sync.dma_start(w2_raw[h][:], w2_rows[:, :, h * (H // 2) : (h + 1) * (H // 2)])
 
         w1_bf = sb("w1_bf", [P, H * PACK], BF16)
-        nc.vector.tensor_copy(
-            w1_bf[:].rearrange("p (t m j) -> p m t j", t=PACK, j=PACK),
-            w1_raw[:].rearrange("p (j m t) -> p m t j", j=PACK, t=PACK),
-        )
+        w1_dst = w1_bf[:].rearrange("p (t m j) -> p m j t", t=PACK, j=PACK)
+        w1_src = w1_raw[:].rearrange("p (j m t) -> p m j t", j=PACK, t=PACK)
+        nc.vector.tensor_copy(w1_dst[:, :W1_SPLIT], w1_src[:, :W1_SPLIT])
+        nc.scalar.copy(w1_dst[:, W1_SPLIT:], w1_src[:, W1_SPLIT:])
         dinv_t = reuse.tile([P, PACK, S], F32, name="dinv_t", offset=8192)
         nc.sync.dma_start(dinv_t[:], dinv.rearrange("(p t) n -> p t n", t=PACK))
         w1_q = sb("w1_q", [P, H], U32)
@@ -99,30 +100,29 @@ def tile_picked_jacobi2_none_p_kernel(
             lists = offs_t[:, h * HALF // PER_COL : (h + 1) * HALF // PER_COL]
             nc.vector.tensor_copy(x_q[:, h * HALF : (h + 1) * HALF], word_win[:].bitcast(U32).indirect(lists))
 
-        stage = sb("stage", [P, (QUARTER + H) * PACK], BF16)
-        w2_bf = stage[:, QUARTER * PACK :]
-        w2_dst = w2_bf.rearrange("p (t m j) -> p m t j", t=PACK, j=PACK)
+        w2_bf = sb("w2_bf", [P, H * PACK], BF16)[:]
+        w2_dst = w2_bf.rearrange("p (t m j) -> p m j t", t=PACK, j=PACK)
         for h in range(2):
             nc.scalar.copy(
                 w2_dst[:, h * (P // 2) : (h + 1) * (P // 2)],
-                w2_raw[h][:].rearrange("p j (m t) -> p m t j", t=PACK),
+                w2_raw[h][:].rearrange("p j (m t) -> p m j t", t=PACK),
             )
         w2_s = sb("w2_s", [P, H], U8)
 
         y_ps = [bank(c, [P, PACK, QUARTER]) for c in range(4)]
         for c in range(4):
+            cols = slice(c * QUARTER, (c + 1) * QUARTER)
             for t in range(PACK):
-                mx(y_ps[c][:, t, :], w1_q, w1_s, t, x_q, x_sc, slice(c * QUARTER, (c + 1) * QUARTER), True, True)
+                mx(y_ps[c][:, t, :], w1_q, w1_s, t, x_q[:, cols], x_sc[:, cols], True, True)
 
         r1 = [bank(4 + t, [P, S]) for t in range(PACK)]
         for t in range(PACK - 1):
-            mx(r1[t][:], w1_q, w1_s, t, x_q, x_sc, slice(0, S), True, False)
+            mx(r1[t][:], w1_q, w1_s, t, x_q[:], x_sc[:], True, False)
 
         z_bf = [
-            keep.tile([P, HALF * PACK], BF16, name="z_bf0", tag="z0_then_w2", align_bytes=64)[:],
-            stage[:, : HALF * PACK],
+            sb("z_bf0", [P, HALF * PACK], BF16)[:],
+            sb("z_bf1", [P, HALF * PACK], BF16)[:],
         ]
-        z_q = sb("z_q", [P, S], U32)
         z_s = sb("z_s", [P, S], U8)
         y_sb = reuse.tile([P, PACK, S], F32, name="y_sb", offset=0)
         gain_b = gain[:].unsqueeze(1).to_broadcast([P, QUARTER, PACK])
@@ -134,52 +134,54 @@ def tile_picked_jacobi2_none_p_kernel(
 
         def quantize_half(codes, scales, values, h):
             cols = slice(h * HALF, (h + 1) * HALF)
-            nc.vector.quantize_mx(out=codes[:, cols].bitcast(FP8X4), scales=scales[:, cols], in_=values)
+            nc.vector.quantize_mx(out=codes.bitcast(FP8X4), scales=scales[:, cols], in_=values)
 
         make_z(0)
         make_z(1)
+        aside = sb("shared", [P, 2 * S], F32)
+        factor, last = aside[:, :S], aside[:, S:]
+        nc.scalar.activation(factor, dinv_t[:, PACK - 1, :], COPY, scale=gain[:, PACK - 1 : PACK])
         make_z(2)
-        quantize_half(z_q, z_s, z_bf[0], 0)
-        w2_q = keep.tile([P, H], U32, name="w2_q", tag="z0_then_w2", align_bytes=64)
-        nc.vector.quantize_mx(out=w2_q[:].bitcast(FP8X4), scales=w2_s[:], in_=w2_bf)
+        z_q = [sb("z_q0", [P, HALF], U32)[:]]
+        quantize_half(z_q[0], z_s, z_bf[0], 0)
         make_z(3)
-        quantize_half(z_q, z_s, z_bf[1], 1)
+        w2_q = sb("z_bf0", [P, H], U32)
+        nc.vector.quantize_mx(out=w2_q[:].bitcast(FP8X4), scales=w2_s[:], in_=w2_bf)
+        z_q.append(sb("w2_bf", [P, HALF], U32)[:])
+        quantize_half(z_q[1], z_s, z_bf[1], 1)
 
         LAST = PACK - 1
         win = [sb("win%d" % t, [P, S], F32) for t in range(PACK)]
-        last = sb("last", [P, S], F32)
 
         def first_product(t, h):
             cols = slice(h * HALF, (h + 1) * HALF)
-            mx(r1[t][:, cols], w2_q, w2_s, t, z_q, z_s, cols, t == LAST, t == LAST or h == 1)
+            mx(r1[t][:, cols], w2_q, w2_s, t, z_q[h], z_s[:, cols], t == LAST, t == LAST or h == 1)
 
         def first_sum(cols):
             nc.vector.tensor_tensor(last[:, cols], r1[LAST][:, cols], y_sb[:, LAST, cols], ADD)
 
-        def first_values(t, cols):
-            rest = r1[t][:, cols] if t < LAST else last[:, cols]
-            nc.vector.scalar_tensor_tensor(win[t][:, cols], rest, gain[:, t : t + 1], dinv_t[:, t, cols], MULT, MULT)
+        def first_values(t):
+            nc.vector.scalar_tensor_tensor(win[t][:], r1[t][:], gain[:, t : t + 1], dinv_t[:, t, :], MULT, MULT)
+
+        def last_values(cols):
+            nc.gpsimd.tensor_tensor(win[LAST][:, cols], last[:, cols], factor[:, cols], MULT)
+
+        first_product(LAST, 0)
+        first_product(0, 0)
+        first_product(0, 1)
+        first_sum(slice(0, HALF))
+        last_values(slice(0, HALF))
+        first_product(LAST, 1)
+        for t in (1, 2):
+            first_product(t, 0)
+            first_product(t, 1)
+        first_values(0)
+        first_sum(slice(HALF, S))
+        last_values(slice(HALF, S))
+        first_values(1)
+        first_values(2)
 
         shared = sb("shared", [P, (2 * PACK - 1) * HALF], BF16)
-        scaled = [sb("scaled", [P, S], F32)[:], shared[:, HALF : HALF + 2 * S].bitcast(F32)]
-
-        def first_values_aside(t):
-            nc.scalar.activation(scaled[t - 1], r1[t][:], COPY, scale=gain[:, t : t + 1])
-            nc.gpsimd.tensor_tensor(win[t][:], scaled[t - 1], dinv_t[:, t, :], MULT)
-
-        for t in (LAST, 1, 0, 2):
-            first_product(t, 0)
-        for t in (1, 0, 2):
-            first_product(t, 1)
-        first_sum(slice(0, HALF))
-        first_values(LAST, slice(0, HALF))
-        first_product(LAST, 1)
-        first_values_aside(1)
-        first_values_aside(2)
-        first_values(0, slice(0, S))
-        first_sum(slice(HALF, S))
-        first_values(LAST, slice(HALF, S))
-
         got0 = sb("got0", [P, PACK, HALF], BF16)
         woven0 = shared[:, (PACK - 1) * HALF :]
         got1 = shared[:, : PACK * HALF].rearrange("p (t n) -> p t n", t=PACK)
@@ -187,48 +189,52 @@ def tile_picked_jacobi2_none_p_kernel(
         z2_q = sb("z2_q", [P, S], U32)
         z2_s = sb("z2_s", [P, S], U8)
 
+        def weave(dst, planes):
+            nc.scalar.copy(
+                dst.rearrange("p (c i t) -> p c t i", i=PACK, t=PACK),
+                planes.rearrange("p t (c i) -> p c t i", i=PACK),
+            )
+
         def fetch(dst, t, h):
             lists = nb_t[:, h * HALF // PER_COL : (h + 1) * HALF // PER_COL]
             nc.vector.tensor_copy(dst, win[t][:].indirect(lists))
 
-        for t in (0, 3, 1, 2):
+        for t in range(PACK):
             fetch(got0[:, t, :], t, 0)
-        nc.scalar.copy(woven0.rearrange("p (n t) -> p n t", t=PACK), got0[:].rearrange("p t n -> p n t"))
+        weave(woven0, got0[:])
         for t in range(PACK - 1):
             fetch(got1[:, t, :], t, 1)
-        quantize_half(z2_q, z2_s, woven0, 0)
+        quantize_half(z2_q[:, :HALF], z2_s, woven0, 0)
         fetch(got1[:, PACK - 1, :], PACK - 1, 1)
-        nc.scalar.copy(woven1[:].rearrange("p (n t) -> p n t", t=PACK), got1.rearrange("p t n -> p n t"))
+        weave(woven1[:], got1)
 
         out_rows = out.rearrange("(p t) n -> p t n", t=PACK)
         r2 = [[bank(2 * h + u, [P, 2, HALF]) for u in range(2)] for h in range(2)]
-        rest2 = [[sb("rest%d%d" % (h, u), [P, 2, HALF], F32) for u in range(2)] for h in range(2)]
+        rest2 = [sb("rest%d" % h, [P, PACK, HALF], F32) for h in range(2)]
 
         def product(h):
             cols = slice(h * HALF, (h + 1) * HALF)
             for t in range(PACK):
-                mx(r2[h][t // 2][:, t % 2, :], w2_q, w2_s, t, z2_q, z2_s, cols, True, True)
+                mx(r2[h][t // 2][:, t % 2, :], w2_q, w2_s, t, z2_q[:, cols], z2_s[:, cols], True, True)
 
-        def subtract(h, u):
+        def subtract(h):
             cols = slice(h * HALF, (h + 1) * HALF)
-            nc.vector.tensor_tensor(rest2[h][u][:], r2[h][u][:], y_sb[:, 2 * u : 2 * u + 2, cols], ADD)
+            for u in range(2):
+                planes = slice(2 * u, 2 * u + 2)
+                nc.vector.tensor_tensor(rest2[h][:, planes], r2[h][u][:], y_sb[:, planes, cols], ADD)
 
-        def finish(engine, res, h, u, lo=0, hi=2):
+        def finish(engine, res, h, planes):
             cols = slice(h * HALF, (h + 1) * HALF)
-            planes = slice(2 * u + lo, 2 * u + hi)
-            engine.tensor_tensor(res[:, lo:hi], rest2[h][u][:, lo:hi], dinv_t[:, planes, cols], MULT)
-            nc.sync.dma_start(out_rows[:, planes, cols], res[:, lo:hi])
+            engine.tensor_tensor(res, rest2[h][:, planes], dinv_t[:, planes, cols], MULT)
+            nc.sync.dma_start(out_rows[:, planes, cols], res)
 
         product(0)
-        subtract(0, 0)
-        subtract(0, 1)
-        quantize_half(z2_q, z2_s, woven1[:], 1)
+        subtract(0)
+        quantize_half(z2_q[:, HALF:], z2_s, woven1[:], 1)
         product(1)
-        finish(nc.vector, sb("woven1", [P, 2, HALF], F32), 0, 0)
-        finish(nc.gpsimd, sb("rest00", [P, 2, HALF], F32), 0, 1)
-        subtract(1, 0)
-        subtract(1, 1)
-        finish(nc.vector, sb("res10", [P, 2, HALF], F32), 1, 0)
-        res11 = sb("res11", [P, 2, HALF], F32)
-        finish(nc.vector, res11, 1, 1, 0, 1)
-        finish(nc.vector, res11, 1, 1, 1, 2)
+        finish(nc.vector, sb("woven1", [P, LAST, HALF], F32)[:], 0, slice(0, LAST))
+        finish(nc.gpsimd, rest2[0][:, 0:1], 0, slice(LAST, PACK))
+        subtract(1)
+        res1 = sb("res1", [P, PACK, HALF], F32)
+        for planes in (slice(0, 2), slice(2, 3), slice(3, 4)):
+            finish(nc.vector, res1[:, planes], 1, planes)

@@ -2,8 +2,8 @@ from contextlib import ExitStack
 
 import concourse.mybir as mybir
 
-K, T, S, H = 512, 2048, 512, 512
-FLOPS = 3 * 2 * 512 * 512 * 512
+T, S, H = 2048, 512, 512
+FLOPS = 3 * 2 * H * H * S
 
 F32 = mybir.dt.float32
 BF16 = mybir.dt.bfloat16
@@ -18,10 +18,29 @@ COPY = mybir.ActivationFunctionType.Copy
 
 P = 128
 PACK = 4
+LAST = PACK - 1
 HALF = S // 2
 QUARTER = S // 4
-PER_COL = 16
-W1_SPLIT = 80
+LIST_ROWS = 16
+BLOCK_ROWS = 8
+QUADRANT = 32
+W1_VECTOR = 80
+
+W2_HALF_BYTES = PACK * (H // 2) * 4
+SCALE_WINDOW_AT = W2_HALF_BYTES - T // 2
+W1_AT = 2 * W2_HALF_BYTES
+
+
+def half(h):
+    return slice(h * HALF, (h + 1) * HALF)
+
+
+def quarter(c):
+    return slice(c * QUARTER, (c + 1) * QUARTER)
+
+
+def list_half(lists, h):
+    return lists[:, h * HALF // LIST_ROWS : (h + 1) * HALF // LIST_ROWS]
 
 
 def tile_picked_jacobi2_none_p_kernel(
@@ -33,39 +52,42 @@ def tile_picked_jacobi2_none_p_kernel(
         reuse = ctx.enter_context(tc.tile_pool(name="reuse", bufs=1))
         psum = ctx.enter_context(tc.psum_pool(name="psum", bufs=1))
 
-        def sb(name, shape, dtype):
-            return keep.tile(shape, dtype, name=name, align_bytes=64)
+        def sb(name, shape, dtype, on=None):
+            return keep.tile(shape, dtype, name=name, tag=on or name, align_bytes=64)
 
         def bank(index, shape):
             return psum.tile(shape, F32, name="bank%d" % index)
 
         def mx(acc, w_codes, w_scales, t, codes, scales, start, stop):
-            rows = slice(t * P, (t + 1) * P)
+            features = slice(t * P, (t + 1) * P)
             nc.tensor.matmul_mx(
                 out=acc,
-                lhsT=w_codes[:, rows].bitcast(FP8X4),
-                lhsT_scale=w_scales[:, rows],
+                lhsT=w_codes[:, features].bitcast(FP8X4),
+                lhsT_scale=w_scales[:, features],
                 rhs=codes.bitcast(FP8X4),
                 rhs_scale=scales,
                 start=start,
                 stop=stop,
             )
 
-        offs_t = keep.tile([P, S // PER_COL], U16, name="offs_t")
-        nb_t = keep.tile([P, S // PER_COL], U16, name="nb_t")
-        scale_win = reuse.tile([P, T], U8, name="scale_win", offset=3072)
+        def quantize(codes, scales, woven):
+            nc.vector.quantize_mx(out=codes.bitcast(FP8X4), scales=scales, in_=woven)
+
+        offs_t = keep.tile([P, S // LIST_ROWS], U16, name="offs_t")
+        nb_t = keep.tile([P, S // LIST_ROWS], U16, name="nb_t")
+        scale_win = reuse.tile([P, T], U8, name="scale_win", offset=SCALE_WINDOW_AT)
         nc.vector.memset(scale_win[:, : T // 2].bitcast(I32), 0)
         nc.gpsimd.memset(scale_win[:, T // 2 :].bitcast(I32), 0)
-        x_sc = sb("x_sc", [P, S], U8)
+        x_s = sb("x_s", [P, S], U8)
 
-        nc.sync.dma_start(offs_t[:], offs)
-        w1_raw = reuse.tile([P, PACK * H], F32, name="w1_raw", offset=8192)
+        w1_raw = reuse.tile([P, PACK * H], F32, name="w1_raw", offset=W1_AT)
         w1_rows = w1.rearrange("(p j) c -> p (j c)", j=PACK)
         nc.sync.dma_start(w1_raw[:, :H], w1_rows[:, :H])
+        nc.sync.dma_start(offs_t[:], offs)
         gn_t = sb("gn_t", [P, PACK], F32)
         nc.sync.dma_start(gn_t[:], gn.rearrange("(p t) o -> p (t o)", t=PACK))
         nc.sync.dma_start(nb_t[:], nb)
-        nc.sync.dma_start(scale_win[0:P:8, :].bitcast(I32), x_scales[0].bitcast(I32))
+        nc.sync.dma_start(scale_win[0:P:BLOCK_ROWS, :].bitcast(I32), x_scales[0].bitcast(I32))
         nc.sync.dma_start(w1_raw[:, H:], w1_rows[:, H:])
         word_win = sb("word_win", [P, T], I32)
         nc.sync.dma_start(word_win[:], x_words[0].rearrange("p n r -> p (n r)").bitcast(I32))
@@ -75,33 +97,34 @@ def tile_picked_jacobi2_none_p_kernel(
 
         scale_got = sb("scale_got", [P, S], U8)
         nc.vector.tensor_copy(scale_got[:], scale_win[:].indirect(offs_t[:]))
-        for c in range(4):
-            queue = nc.sync if c % 2 else nc.scalar
-            queue.dma_start(x_sc[c:P:32, :].bitcast(I32), scale_got[8 * c : P : 32, :].bitcast(I32))
+        for r in range(QUADRANT // BLOCK_ROWS):
+            queue = nc.sync if r % 2 else nc.scalar
+            queue.dma_start(x_s[r:P:QUADRANT, :].bitcast(I32), scale_got[BLOCK_ROWS * r : P : QUADRANT, :].bitcast(I32))
 
         w2_rows = w2.rearrange("(p j) c -> p j c", j=PACK)
-        w2_raw = [reuse.tile([P, PACK, H // 2], F32, name="w2_raw%d" % h, offset=4096 * h) for h in range(2)]
+        w2_raw = [
+            reuse.tile([P, PACK, H // 2], F32, name="w2_raw%d" % h, offset=W2_HALF_BYTES * h) for h in range(2)
+        ]
         for h in range(2):
             nc.sync.dma_start(w2_raw[h][:], w2_rows[:, :, h * (H // 2) : (h + 1) * (H // 2)])
 
         w1_bf = sb("w1_bf", [P, H * PACK], BF16)
         w1_dst = w1_bf[:].rearrange("p (t m j) -> p m j t", t=PACK, j=PACK)
         w1_src = w1_raw[:].rearrange("p (j m t) -> p m j t", j=PACK, t=PACK)
-        nc.vector.tensor_copy(w1_dst[:, :W1_SPLIT], w1_src[:, :W1_SPLIT])
-        nc.scalar.copy(w1_dst[:, W1_SPLIT:], w1_src[:, W1_SPLIT:])
-        dinv_t = reuse.tile([P, PACK, S], F32, name="dinv_t", offset=8192)
+        nc.vector.tensor_copy(w1_dst[:, :W1_VECTOR], w1_src[:, :W1_VECTOR])
+        nc.scalar.copy(w1_dst[:, W1_VECTOR:], w1_src[:, W1_VECTOR:])
+        dinv_t = reuse.tile([P, PACK, S], F32, name="dinv_t", offset=W1_AT)
         nc.sync.dma_start(dinv_t[:], dinv.rearrange("(p t) n -> p t n", t=PACK))
         w1_q = sb("w1_q", [P, H], U32)
         w1_s = sb("w1_s", [P, H], U8)
-        nc.vector.quantize_mx(out=w1_q[:].bitcast(FP8X4), scales=w1_s[:], in_=w1_bf[:])
+        quantize(w1_q[:], w1_s[:], w1_bf[:])
 
         x_q = sb("x_q", [P, S], U32)
         for h in range(2):
-            lists = offs_t[:, h * HALF // PER_COL : (h + 1) * HALF // PER_COL]
-            nc.vector.tensor_copy(x_q[:, h * HALF : (h + 1) * HALF], word_win[:].bitcast(U32).indirect(lists))
+            nc.vector.tensor_copy(x_q[:, half(h)], word_win[:].bitcast(U32).indirect(list_half(offs_t, h)))
 
-        w2_bf = sb("w2_bf", [P, H * PACK], BF16)[:]
-        w2_dst = w2_bf.rearrange("p (t m j) -> p m j t", t=PACK, j=PACK)
+        w2_bf = sb("w2_bf", [P, H * PACK], BF16)
+        w2_dst = w2_bf[:].rearrange("p (t m j) -> p m j t", t=PACK, j=PACK)
         for h in range(2):
             nc.scalar.copy(
                 w2_dst[:, h * (P // 2) : (h + 1) * (P // 2)],
@@ -111,130 +134,115 @@ def tile_picked_jacobi2_none_p_kernel(
 
         y_ps = [bank(c, [P, PACK, QUARTER]) for c in range(4)]
         for c in range(4):
-            cols = slice(c * QUARTER, (c + 1) * QUARTER)
             for t in range(PACK):
-                mx(y_ps[c][:, t, :], w1_q, w1_s, t, x_q[:, cols], x_sc[:, cols], True, True)
+                mx(y_ps[c][:, t, :], w1_q, w1_s, t, x_q[:, quarter(c)], x_s[:, quarter(c)], True, True)
 
-        r1 = [bank(4 + t, [P, S]) for t in range(PACK)]
-        for t in range(PACK - 1):
-            mx(r1[t][:], w1_q, w1_s, t, x_q[:], x_sc[:], True, False)
+        sweep1 = [bank(4 + t, [P, S]) for t in range(PACK)]
+        for t in range(LAST):
+            mx(sweep1[t][:], w1_q, w1_s, t, x_q[:], x_s[:], True, False)
 
-        z_bf = [
-            sb("z_bf0", [P, HALF * PACK], BF16)[:],
-            sb("z_bf1", [P, HALF * PACK], BF16)[:],
-        ]
+        z_bf = [sb("z_bf%d" % h, [P, HALF * PACK], BF16) for h in range(2)]
         z_s = sb("z_s", [P, S], U8)
         y_sb = reuse.tile([P, PACK, S], F32, name="y_sb", offset=0)
-        gain_b = gain[:].unsqueeze(1).to_broadcast([P, QUARTER, PACK])
+        gain_woven = gain[:].unsqueeze(1).to_broadcast([P, QUARTER, PACK])
 
         def make_z(c):
-            dst = z_bf[c // 2][:, c % 2 * QUARTER * PACK : (c % 2 + 1) * QUARTER * PACK].rearrange("p (n t) -> p n t", t=PACK)
-            nc.vector.tensor_tensor(dst, y_ps[c][:].rearrange("p t n -> p n t"), gain_b, MULT)
-            nc.scalar.copy(y_sb[:, :, c * QUARTER : (c + 1) * QUARTER], y_ps[c][:])
-
-        def quantize_half(codes, scales, values, h):
-            cols = slice(h * HALF, (h + 1) * HALF)
-            nc.vector.quantize_mx(out=codes.bitcast(FP8X4), scales=scales[:, cols], in_=values)
+            dst = z_bf[c // 2][:, c % 2 * QUARTER * PACK : (c % 2 + 1) * QUARTER * PACK]
+            nc.vector.tensor_tensor(
+                dst.rearrange("p (n t) -> p n t", t=PACK), y_ps[c][:].rearrange("p t n -> p n t"), gain_woven, MULT
+            )
+            nc.scalar.copy(y_sb[:, :, quarter(c)], y_ps[c][:])
 
         make_z(0)
         make_z(1)
-        aside = sb("shared", [P, 2 * S], F32)
-        factor, last = aside[:, :S], aside[:, S:]
-        nc.scalar.activation(factor, dinv_t[:, PACK - 1, :], COPY, scale=gain[:, PACK - 1 : PACK])
+        last_plane = sb("last_plane", [P, 2 * S], F32)
+        last_factor, last_sum = last_plane[:, :S], last_plane[:, S:]
+        nc.scalar.activation(last_factor, dinv_t[:, LAST, :], COPY, scale=gain[:, LAST:PACK])
         make_z(2)
-        z_q = [sb("z_q0", [P, HALF], U32)[:]]
-        quantize_half(z_q[0], z_s, z_bf[0], 0)
+        z_q = [sb("z_q0", [P, HALF], U32)]
+        quantize(z_q[0][:], z_s[:, half(0)], z_bf[0][:])
         make_z(3)
-        w2_q = sb("z_bf0", [P, H], U32)
-        nc.vector.quantize_mx(out=w2_q[:].bitcast(FP8X4), scales=w2_s[:], in_=w2_bf)
-        z_q.append(sb("w2_bf", [P, HALF], U32)[:])
-        quantize_half(z_q[1], z_s, z_bf[1], 1)
+        w2_q = sb("w2_q", [P, H], U32, on="z_bf0")
+        quantize(w2_q[:], w2_s[:], w2_bf[:])
+        z_q.append(sb("z_q1", [P, HALF], U32, on="w2_bf"))
+        quantize(z_q[1][:], z_s[:, half(1)], z_bf[1][:])
 
-        LAST = PACK - 1
         win = [sb("win%d" % t, [P, S], F32) for t in range(PACK)]
 
         def first_product(t, h):
-            cols = slice(h * HALF, (h + 1) * HALF)
-            mx(r1[t][:, cols], w2_q, w2_s, t, z_q[h], z_s[:, cols], t == LAST, t == LAST or h == 1)
-
-        def first_sum(cols):
-            nc.vector.tensor_tensor(last[:, cols], r1[LAST][:, cols], y_sb[:, LAST, cols], ADD)
+            mx(sweep1[t][:, half(h)], w2_q, w2_s, t, z_q[h][:], z_s[:, half(h)], t == LAST, t == LAST or h == 1)
 
         def first_values(t):
-            nc.vector.scalar_tensor_tensor(win[t][:], r1[t][:], gain[:, t : t + 1], dinv_t[:, t, :], MULT, MULT)
+            nc.vector.scalar_tensor_tensor(win[t][:], sweep1[t][:], gain[:, t : t + 1], dinv_t[:, t, :], MULT, MULT)
 
-        def last_values(cols):
-            nc.gpsimd.tensor_tensor(win[LAST][:, cols], last[:, cols], factor[:, cols], MULT)
+        def last_values(h):
+            nc.vector.tensor_tensor(last_sum[:, half(h)], sweep1[LAST][:, half(h)], y_sb[:, LAST, half(h)], ADD)
+            nc.gpsimd.tensor_tensor(win[LAST][:, half(h)], last_sum[:, half(h)], last_factor[:, half(h)], MULT)
 
         first_product(LAST, 0)
         first_product(0, 0)
         first_product(0, 1)
-        first_sum(slice(0, HALF))
-        last_values(slice(0, HALF))
+        last_values(0)
         first_product(LAST, 1)
-        for t in (1, 2):
+        for t in range(1, LAST):
             first_product(t, 0)
             first_product(t, 1)
         first_values(0)
-        first_sum(slice(HALF, S))
-        last_values(slice(HALF, S))
-        first_values(1)
-        first_values(2)
+        last_values(1)
+        for t in range(1, LAST):
+            first_values(t)
 
-        shared = sb("shared", [P, (2 * PACK - 1) * HALF], BF16)
+        second = sb("second", [P, (PACK + LAST) * HALF], BF16, on="last_plane")
         got0 = sb("got0", [P, PACK, HALF], BF16)
-        woven0 = shared[:, (PACK - 1) * HALF :]
-        got1 = shared[:, : PACK * HALF].rearrange("p (t n) -> p t n", t=PACK)
+        woven0 = second[:, LAST * HALF :]
+        got1 = second[:, : PACK * HALF].rearrange("p (t n) -> p t n", t=PACK)
         woven1 = sb("woven1", [P, PACK * HALF], BF16)
         z2_q = sb("z2_q", [P, S], U32)
         z2_s = sb("z2_s", [P, S], U8)
 
         def weave(dst, planes):
             nc.scalar.copy(
-                dst.rearrange("p (c i t) -> p c t i", i=PACK, t=PACK),
-                planes.rearrange("p t (c i) -> p c t i", i=PACK),
+                dst.rearrange("p (g i t) -> p g t i", i=PACK, t=PACK),
+                planes.rearrange("p t (g i) -> p g t i", i=PACK),
             )
 
-        def fetch(dst, t, h):
-            lists = nb_t[:, h * HALF // PER_COL : (h + 1) * HALF // PER_COL]
-            nc.vector.tensor_copy(dst, win[t][:].indirect(lists))
+        def fetch(got, t, h):
+            nc.vector.tensor_copy(got[:, t, :], win[t][:].indirect(list_half(nb_t, h)))
 
         for t in range(PACK):
-            fetch(got0[:, t, :], t, 0)
+            fetch(got0, t, 0)
         weave(woven0, got0[:])
-        for t in range(PACK - 1):
-            fetch(got1[:, t, :], t, 1)
-        quantize_half(z2_q[:, :HALF], z2_s, woven0, 0)
-        fetch(got1[:, PACK - 1, :], PACK - 1, 1)
+        for t in range(LAST):
+            fetch(got1, t, 1)
+        quantize(z2_q[:, half(0)], z2_s[:, half(0)], woven0)
+        fetch(got1, LAST, 1)
         weave(woven1[:], got1)
 
         out_rows = out.rearrange("(p t) n -> p t n", t=PACK)
-        r2 = [[bank(2 * h + u, [P, 2, HALF]) for u in range(2)] for h in range(2)]
-        rest2 = [sb("rest%d" % h, [P, PACK, HALF], F32) for h in range(2)]
+        sweep2 = [[bank(2 * h + u, [P, 2, HALF]) for u in range(2)] for h in range(2)]
+        sums = [sb("sums%d" % h, [P, PACK, HALF], F32) for h in range(2)]
 
-        def product(h):
-            cols = slice(h * HALF, (h + 1) * HALF)
+        def second_product(h):
             for t in range(PACK):
-                mx(r2[h][t // 2][:, t % 2, :], w2_q, w2_s, t, z2_q[:, cols], z2_s[:, cols], True, True)
+                mx(sweep2[h][t // 2][:, t % 2, :], w2_q, w2_s, t, z2_q[:, half(h)], z2_s[:, half(h)], True, True)
 
-        def subtract(h):
-            cols = slice(h * HALF, (h + 1) * HALF)
+        def add_y(h):
             for u in range(2):
                 planes = slice(2 * u, 2 * u + 2)
-                nc.vector.tensor_tensor(rest2[h][:, planes], r2[h][u][:], y_sb[:, planes, cols], ADD)
+                nc.vector.tensor_tensor(sums[h][:, planes], sweep2[h][u][:], y_sb[:, planes, half(h)], ADD)
 
-        def finish(engine, res, h, planes):
-            cols = slice(h * HALF, (h + 1) * HALF)
-            engine.tensor_tensor(res, rest2[h][:, planes], dinv_t[:, planes, cols], MULT)
-            nc.sync.dma_start(out_rows[:, planes, cols], res)
+        def finish(engine, result, h, planes):
+            engine.tensor_tensor(result, sums[h][:, planes], dinv_t[:, planes, half(h)], MULT)
+            nc.sync.dma_start(out_rows[:, planes, half(h)], result)
 
-        product(0)
-        subtract(0)
-        quantize_half(z2_q[:, HALF:], z2_s, woven1[:], 1)
-        product(1)
-        finish(nc.vector, sb("woven1", [P, LAST, HALF], F32)[:], 0, slice(0, LAST))
-        finish(nc.gpsimd, rest2[0][:, 0:1], 0, slice(LAST, PACK))
-        subtract(1)
-        res1 = sb("res1", [P, PACK, HALF], F32)
-        for planes in (slice(0, 2), slice(2, 3), slice(3, 4)):
-            finish(nc.vector, res1[:, planes], 1, planes)
+        second_product(0)
+        add_y(0)
+        quantize(z2_q[:, half(1)], z2_s[:, half(1)], woven1[:])
+        second_product(1)
+        result0 = sb("result0", [P, LAST, HALF], F32, on="woven1")
+        finish(nc.vector, result0[:], 0, slice(0, LAST))
+        finish(nc.gpsimd, sums[0][:, 0:1], 0, slice(LAST, PACK))
+        add_y(1)
+        result1 = sb("result1", [P, PACK, HALF], F32)
+        for planes in (slice(0, 2), slice(2, LAST), slice(LAST, PACK)):
+            finish(nc.vector, result1[:, planes], 1, planes)

from contextlib import ExitStack

import concourse.mybir as mybir

T, S, H = 2048, 512, 512
FLOPS = 3 * 2 * H * H * S

F32 = mybir.dt.float32
BF16 = mybir.dt.bfloat16
I32 = mybir.dt.int32
U32 = mybir.dt.uint32
U16 = mybir.dt.uint16
U8 = mybir.dt.uint8
FP8X4 = mybir.dt.float8_e4m3fn_x4
MULT = mybir.AluOpType.mult
ADD = mybir.AluOpType.add
COPY = mybir.ActivationFunctionType.Copy

P = 128
PACK = 4
LAST = PACK - 1
HALF = S // 2
QUARTER = S // 4
LIST_ROWS = 16
BLOCK_ROWS = 8
QUADRANT = 32
W1_VECTOR = 80

W2_HALF_BYTES = PACK * (H // 2) * 4
SCALE_WINDOW_AT = W2_HALF_BYTES - T // 2
W1_AT = 2 * W2_HALF_BYTES


def half(h):
    return slice(h * HALF, (h + 1) * HALF)


def quarter(c):
    return slice(c * QUARTER, (c + 1) * QUARTER)


def list_half(lists, h):
    return lists[:, h * HALF // LIST_ROWS : (h + 1) * HALF // LIST_ROWS]


def tile_picked_jacobi2_none_p_kernel(
    tc, x_words, x_scales, w1, gn, dinv, w2, offs, nb, out
):
    nc = tc.nc
    with ExitStack() as ctx:
        keep = ctx.enter_context(tc.tile_pool(name="keep", bufs=1))
        reuse = ctx.enter_context(tc.tile_pool(name="reuse", bufs=1))
        psum = ctx.enter_context(tc.psum_pool(name="psum", bufs=1))

        def sb(name, shape, dtype, on=None):
            return keep.tile(shape, dtype, name=name, tag=on or name, align_bytes=64)

        def bank(index, shape):
            return psum.tile(shape, F32, name="bank%d" % index)

        def mx(acc, w_codes, w_scales, t, codes, scales, start, stop):
            features = slice(t * P, (t + 1) * P)
            nc.tensor.matmul_mx(
                out=acc,
                lhsT=w_codes[:, features].bitcast(FP8X4),
                lhsT_scale=w_scales[:, features],
                rhs=codes.bitcast(FP8X4),
                rhs_scale=scales,
                start=start,
                stop=stop,
            )

        def quantize(codes, scales, woven):
            nc.vector.quantize_mx(out=codes.bitcast(FP8X4), scales=scales, in_=woven)

        offs_t = keep.tile([P, S // LIST_ROWS], U16, name="offs_t")
        nb_t = keep.tile([P, S // LIST_ROWS], U16, name="nb_t")
        scale_win = reuse.tile([P, T], U8, name="scale_win", offset=SCALE_WINDOW_AT)
        nc.vector.memset(scale_win[:, : T // 2].bitcast(I32), 0)
        nc.gpsimd.memset(scale_win[:, T // 2 :].bitcast(I32), 0)
        x_s = sb("x_s", [P, S], U8)

        w1_raw = reuse.tile([P, PACK * H], F32, name="w1_raw", offset=W1_AT)
        w1_rows = w1.rearrange("(p j) c -> p (j c)", j=PACK)
        nc.sync.dma_start(w1_raw[:, :H], w1_rows[:, :H])
        nc.sync.dma_start(offs_t[:], offs)
        gn_t = sb("gn_t", [P, PACK], F32)
        nc.sync.dma_start(gn_t[:], gn.rearrange("(p t) o -> p (t o)", t=PACK))
        nc.sync.dma_start(nb_t[:], nb)
        nc.sync.dma_start(scale_win[0:P:BLOCK_ROWS, :].bitcast(I32), x_scales[0].bitcast(I32))
        nc.sync.dma_start(w1_raw[:, H:], w1_rows[:, H:])
        word_win = sb("word_win", [P, T], I32)
        nc.sync.dma_start(word_win[:], x_words[0].rearrange("p n r -> p (n r)").bitcast(I32))

        gain = sb("gain", [P, PACK], F32)
        nc.scalar.activation(gain[:], gn_t[:], COPY, scale=-0.5)

        scale_got = sb("scale_got", [P, S], U8)
        nc.vector.tensor_copy(scale_got[:], scale_win[:].indirect(offs_t[:]))
        for r in range(QUADRANT // BLOCK_ROWS):
            queue = nc.sync if r % 2 else nc.scalar
            queue.dma_start(x_s[r:P:QUADRANT, :].bitcast(I32), scale_got[BLOCK_ROWS * r : P : QUADRANT, :].bitcast(I32))

        w2_rows = w2.rearrange("(p j) c -> p j c", j=PACK)
        w2_raw = [
            reuse.tile([P, PACK, H // 2], F32, name="w2_raw%d" % h, offset=W2_HALF_BYTES * h) for h in range(2)
        ]
        for h in range(2):
            nc.sync.dma_start(w2_raw[h][:], w2_rows[:, :, h * (H // 2) : (h + 1) * (H // 2)])

        w1_bf = sb("w1_bf", [P, H * PACK], BF16)
        w1_dst = w1_bf[:].rearrange("p (t m j) -> p m j t", t=PACK, j=PACK)
        w1_src = w1_raw[:].rearrange("p (j m t) -> p m j t", j=PACK, t=PACK)
        nc.vector.tensor_copy(w1_dst[:, :W1_VECTOR], w1_src[:, :W1_VECTOR])
        nc.scalar.copy(w1_dst[:, W1_VECTOR:], w1_src[:, W1_VECTOR:])
        dinv_t = reuse.tile([P, PACK, S], F32, name="dinv_t", offset=W1_AT)
        nc.sync.dma_start(dinv_t[:], dinv.rearrange("(p t) n -> p t n", t=PACK))
        w1_q = sb("w1_q", [P, H], U32)
        w1_s = sb("w1_s", [P, H], U8)
        quantize(w1_q[:], w1_s[:], w1_bf[:])

        x_q = sb("x_q", [P, S], U32)
        for h in range(2):
            nc.vector.tensor_copy(x_q[:, half(h)], word_win[:].bitcast(U32).indirect(list_half(offs_t, h)))

        w2_bf = sb("w2_bf", [P, H * PACK], BF16)
        w2_dst = w2_bf[:].rearrange("p (t m j) -> p m j t", t=PACK, j=PACK)
        for h in range(2):
            nc.scalar.copy(
                w2_dst[:, h * (P // 2) : (h + 1) * (P // 2)],
                w2_raw[h][:].rearrange("p j (m t) -> p m j t", t=PACK),
            )
        w2_s = sb("w2_s", [P, H], U8)

        y_ps = [bank(c, [P, PACK, QUARTER]) for c in range(4)]
        for c in range(4):
            for t in range(PACK):
                mx(y_ps[c][:, t, :], w1_q, w1_s, t, x_q[:, quarter(c)], x_s[:, quarter(c)], True, True)

        sweep1 = [bank(4 + t, [P, S]) for t in range(PACK)]
        for t in range(LAST):
            mx(sweep1[t][:], w1_q, w1_s, t, x_q[:], x_s[:], True, False)

        z_bf = [sb("z_bf%d" % h, [P, HALF * PACK], BF16) for h in range(2)]
        z_s = sb("z_s", [P, S], U8)
        y_sb = reuse.tile([P, PACK, S], F32, name="y_sb", offset=0)
        gain_woven = gain[:].unsqueeze(1).to_broadcast([P, QUARTER, PACK])

        def make_z(c):
            dst = z_bf[c // 2][:, c % 2 * QUARTER * PACK : (c % 2 + 1) * QUARTER * PACK]
            nc.vector.tensor_tensor(
                dst.rearrange("p (n t) -> p n t", t=PACK), y_ps[c][:].rearrange("p t n -> p n t"), gain_woven, MULT
            )
            nc.scalar.copy(y_sb[:, :, quarter(c)], y_ps[c][:])

        make_z(0)
        make_z(1)
        last_plane = sb("last_plane", [P, 2 * S], F32)
        last_factor, last_sum = last_plane[:, :S], last_plane[:, S:]
        nc.scalar.activation(last_factor, dinv_t[:, LAST, :], COPY, scale=gain[:, LAST:PACK])
        make_z(2)
        z_q = [sb("z_q0", [P, HALF], U32)]
        quantize(z_q[0][:], z_s[:, half(0)], z_bf[0][:])
        make_z(3)
        w2_q = sb("w2_q", [P, H], U32, on="z_bf0")
        quantize(w2_q[:], w2_s[:], w2_bf[:])
        z_q.append(sb("z_q1", [P, HALF], U32, on="w2_bf"))
        quantize(z_q[1][:], z_s[:, half(1)], z_bf[1][:])

        win = [sb("win%d" % t, [P, S], F32) for t in range(PACK)]

        def first_product(t, h):
            mx(sweep1[t][:, half(h)], w2_q, w2_s, t, z_q[h][:], z_s[:, half(h)], t == LAST, t == LAST or h == 1)

        def first_values(t):
            nc.vector.scalar_tensor_tensor(win[t][:], sweep1[t][:], gain[:, t : t + 1], dinv_t[:, t, :], MULT, MULT)

        def last_values(h):
            nc.vector.tensor_tensor(last_sum[:, half(h)], sweep1[LAST][:, half(h)], y_sb[:, LAST, half(h)], ADD)
            nc.gpsimd.tensor_tensor(win[LAST][:, half(h)], last_sum[:, half(h)], last_factor[:, half(h)], MULT)

        first_product(LAST, 0)
        first_product(0, 0)
        first_product(0, 1)
        last_values(0)
        first_product(LAST, 1)
        for t in range(1, LAST):
            first_product(t, 0)
            first_product(t, 1)
        first_values(0)
        last_values(1)
        for t in range(1, LAST):
            first_values(t)

        second = sb("second", [P, (PACK + LAST) * HALF], BF16, on="last_plane")
        got0 = sb("got0", [P, PACK, HALF], BF16)
        woven0 = second[:, LAST * HALF :]
        got1 = second[:, : PACK * HALF].rearrange("p (t n) -> p t n", t=PACK)
        woven1 = sb("woven1", [P, PACK * HALF], BF16)
        z2_q = sb("z2_q", [P, S], U32)
        z2_s = sb("z2_s", [P, S], U8)

        def weave(dst, planes):
            nc.scalar.copy(
                dst.rearrange("p (g i t) -> p g t i", i=PACK, t=PACK),
                planes.rearrange("p t (g i) -> p g t i", i=PACK),
            )

        def fetch(got, t, h):
            nc.vector.tensor_copy(got[:, t, :], win[t][:].indirect(list_half(nb_t, h)))

        for t in range(PACK):
            fetch(got0, t, 0)
        weave(woven0, got0[:])
        for t in range(LAST):
            fetch(got1, t, 1)
        quantize(z2_q[:, half(0)], z2_s[:, half(0)], woven0)
        fetch(got1, LAST, 1)
        weave(woven1[:], got1)

        out_rows = out.rearrange("(p t) n -> p t n", t=PACK)
        sweep2 = [[bank(2 * h + u, [P, 2, HALF]) for u in range(2)] for h in range(2)]
        sums = [sb("sums%d" % h, [P, PACK, HALF], F32) for h in range(2)]

        def second_product(h):
            for t in range(PACK):
                mx(sweep2[h][t // 2][:, t % 2, :], w2_q, w2_s, t, z2_q[:, half(h)], z2_s[:, half(h)], True, True)

        def add_y(h):
            for u in range(2):
                planes = slice(2 * u, 2 * u + 2)
                nc.vector.tensor_tensor(sums[h][:, planes], sweep2[h][u][:], y_sb[:, planes, half(h)], ADD)

        def finish(engine, result, h, planes):
            engine.tensor_tensor(result, sums[h][:, planes], dinv_t[:, planes, half(h)], MULT)
            nc.sync.dma_start(out_rows[:, planes, half(h)], result)

        second_product(0)
        add_y(0)
        quantize(z2_q[:, half(1)], z2_s[:, half(1)], woven1[:])
        second_product(1)
        result0 = sb("result0", [P, LAST, HALF], F32, on="woven1")
        finish(nc.vector, result0[:], 0, slice(0, LAST))
        finish(nc.gpsimd, sums[0][:, 0:1], 0, slice(LAST, PACK))
        add_y(1)
        result1 = sb("result1", [P, PACK, HALF], F32)
        for planes in (slice(0, 2), slice(2, LAST), slice(LAST, PACK)):
            finish(nc.vector, result1[:, planes], 1, planes)
